import numpy as np
import ml_dtypes


def mxq(x, axis, fmt="e4m3"):
    dtype, down = {"e4m3": (ml_dtypes.float8_e4m3fn, 7), "e5m2": (ml_dtypes.float8_e5m2, 14)}[fmt]
    v = np.moveaxis(np.asarray(x, np.float32).astype(ml_dtypes.bfloat16).astype(np.float64), axis, -1)
    blocks = v.reshape(v.shape[:-1] + (-1, 32))
    amax = np.abs(blocks).max(-1, keepdims=True)
    byte = np.maximum(np.where(amax > 0, np.frexp(amax)[1] - 1 + 127, 0) - down, 1)
    scale = np.exp2(byte - 127.0)
    codes = (blocks / scale).astype(np.float32).astype(dtype).astype(np.float64)
    return np.moveaxis((codes * scale).reshape(v.shape), -1, axis)


WIDE = False


def mx_kscale(k):
    if not WIDE:
        return np.ones(k)
    levels = np.array([30, -30])
    if k % 512:
        return np.exp2(np.random.permutation(np.resize(levels, k // 32))).repeat(32)
    a = np.empty((k // 512, 16))
    for p in range(k // 512):
        a[p, :8] = np.random.permutation(np.resize(levels, 8))
        for g in range(8):
            far = levels[np.abs(levels - a[p, g]) >= 10]
            a[p, g + 8] = far[np.random.randint(len(far))]
    return np.exp2(a.ravel()).repeat(32)


def f64(x):
    return np.asarray(x).astype(np.float64)


def striped(idx):
    return np.tile(np.asarray(idx).reshape(-1, 16).T, (8, 1)).astype(np.uint16)


def unstriped(offs):
    return offs[:16].T.reshape(-1).astype(np.int64)


E2M1 = np.array([0.0, 0.5, 1.0, 1.5, 2.0, 3.0, 4.0, 6.0, -0.0, -0.5, -1.0, -1.5, -2.0, -3.0, -4.0, -6.0])


def pack_weight(w, fmt):
    k, n = w.shape
    w = f64(np.asarray(w, np.float32).astype(ml_dtypes.bfloat16)).reshape(k // 32, 32, n)
    amax = np.abs(w).max(1)
    if fmt in ("e4m3", "e5m2"):
        byte = np.frexp(amax)[1] - 1 + 127 - (7 if fmt == "e4m3" else 14)
    else:
        mant, ex = np.frexp(amax / 6.0)
        byte = np.where(mant > 0.5, ex, ex - 1) + 127
    byte = np.clip(np.where(amax > 0, byte, 1), 1, 254)
    scaled = (w * np.exp2(127.0 - byte)[:, None, :]).reshape(k, n).astype(np.float32)
    by_word = np.ascontiguousarray(scaled.reshape(k // 512, 128, 4, n).transpose(0, 1, 3, 2))
    if fmt in ("e4m3", "e5m2"):
        words = by_word.astype(ml_dtypes.float8_e4m3fn if fmt == "e4m3" else ml_dtypes.float8_e5m2).view(np.uint8)
    else:
        c = by_word.astype(ml_dtypes.float4_e2m1fn).view(np.uint8) & 0xF
        words = (c[..., 0::2] | (c[..., 1::2] << 4)).reshape(k // 512, 128, 2 * n)
    return np.ascontiguousarray(words), np.ascontiguousarray(byte.astype(np.uint8).reshape(k // 512, 16, n))


def unpack_weight(words, scales, fmt):
    g, _, n = scales.shape
    words = np.ascontiguousarray(words).reshape(g, 128, n, -1)
    if fmt in ("e4m3", "e5m2"):
        vals = words.view(ml_dtypes.float8_e4m3fn if fmt == "e4m3" else ml_dtypes.float8_e5m2).astype(np.float64)
    else:
        nib = np.empty((g, 128, n, 4), np.uint8)
        nib[..., 0::2] = words & 0xF
        nib[..., 1::2] = words >> 4
        vals = E2M1[nib]
    vals = vals * np.repeat(np.exp2(scales.astype(np.float64) - 127.0), 8, axis=1)[..., None]
    return vals.transpose(0, 1, 3, 2).reshape(g * 512, n)


K, T, J, R, O, N, Z = 1024, 1024, 256, 512, 128, 256, 512


def setup_inputs():
    n = np.random.standard_normal
    idx = np.random.permutation(T)[:J]
    idx2 = np.random.permutation(T)[:J]
    idx3 = np.random.permutation(J)[:O]
    idx4 = np.random.permutation(Z)[:O]
    fk = mx_kscale(K)
    fr = mx_kscale(R)
    wp = pack_weight(n((K, R)) * 1 / np.sqrt(K) * fk[:, None] * fr, "e5m2")
    return {
        "xf": (n((K, T))).astype(np.float32),
        "fk": (np.random.uniform(0.5, 2.0, (K, 1)) / fk[:, None]).astype(np.float32),
        "w_words": wp[0],
        "w_scales": wp[1],
        "wb": (n((R, N)) * 1 / np.sqrt(R) / fr[:, None]).astype(np.float32),
        "tz": (n((N, Z))).astype(np.float32),
        "offs": striped(idx),
        "offs2": striped(idx2),
        "offs3": striped(idx3),
        "offs4": striped(idx4),
    }


def reference(xf, fk, w_words, w_scales, wb, tz, offs, offs2, offs3, offs4):
    idx = unstriped(offs)
    idx2 = unstriped(offs2)
    idx3 = unstriped(offs3)
    idx4 = unstriped(offs4)
    wu = unpack_weight(w_words, w_scales, "e5m2")
    u = (f64(xf)[:, idx] - f64(xf)[:, idx2]) * f64(fk)
    uq = mxq(u, 0, "e4m3")
    a = wu.T @ uq
    ha = np.maximum(a, 0.0)
    hid = ha[:, idx3]
    wbq = mxq(f64(wb), 0, "e5m2")
    hidq = mxq(hid, 0, "e5m2")
    p = wbq.T @ hidq
    y = p * f64(tz)[:, idx4]
    return y

@@ -1,0 +1,163 @@
+from contextlib import ExitStack
+
+import concourse.mybir as mybir
+
+K, T, J, R, O, N, Z = 1024, 1024, 256, 512, 128, 256, 512
+FLOPS = 2 * K * R * J + 2 * R * N * O
+
+F32 = mybir.dt.float32
+BF16 = mybir.dt.bfloat16
+I32 = mybir.dt.int32
+U32 = mybir.dt.uint32
+U16 = mybir.dt.uint16
+U8 = mybir.dt.uint8
+E4X4 = mybir.dt.float8_e4m3fn_x4
+E5X4 = mybir.dt.float8_e5m2_x4
+MULT = mybir.AluOpType.mult
+SUB = mybir.AluOpType.subtract
+COPY = mybir.ActivationFunctionType.Copy
+RELU = mybir.ActivationFunctionType.Relu
+
+P = 128
+PACK = 4
+PASSES = K // (P * PACK)
+HALVES = N // P
+ON_SCALAR = (1, 2, 3, 4, 5)
+
+
+def tile_list_pickgaps_relooked_timeslook_kernel(tc, xf, fk, w_words, w_scales, wb, tz, offs, offs2, offs3, offs4, out):
+    nc = tc.nc
+    with ExitStack() as ctx:
+        keep = ctx.enter_context(tc.tile_pool(name="keep", bufs=1))
+        psum = ctx.enter_context(tc.psum_pool(name="psum", bufs=1))
+
+        list1 = keep.tile([P, J // 16], U16, name="list1")
+        list2 = keep.tile([P, J // 16], U16, name="list2")
+        list3 = keep.tile([P, O // 16], U16, name="list3")
+        list4 = keep.tile([P, O // 16], U16, name="list4")
+        fk_sb = keep.tile([P, PASSES, PACK], F32, name="fk_sb")
+        w_raw = keep.tile([P, PASSES, R], U32, name="w_raw")
+        ws_raw = keep.tile([P, PASSES, R], U8, name="ws_raw")
+        ws_rows = keep.tile([P, PASSES, R // 4], I32, name="ws_rows")
+        wb_raw = keep.tile([P, PACK, N], F32, name="wb_raw")
+        tz_sb = keep.tile([P, HALVES, Z], F32, name="tz_sb")
+        planes = [keep.tile([P, T], F32, name=f"plane{q}", tag=f"plane{q}", align_bytes=64) for q in range(PASSES * PACK)]
+        x_rows = xf.rearrange("(z p t) c -> z t p c", z=PASSES, t=PACK)
+
+        def load_plane(q):
+            nc.sync.dma_start(out=planes[q][:], in_=x_rows[q // PACK, q % PACK])
+
+        def load_scale_rows(quad):
+            nc.sync.dma_start(
+                out=ws_rows[32 * quad : 32 * quad + 4],
+                in_=w_scales[:, 4 * quad : 4 * quad + 4, :].rearrange("z q c -> q z c").bitcast(I32),
+            )
+
+        load_plane(0)
+        nc.sync.dma_start(list2[:], offs2)
+        nc.sync.dma_start(list1[:], offs)
+        load_plane(1)
+        nc.sync.dma_start(out=fk_sb[:], in_=fk.rearrange("(z p t) one -> p z (t one)", z=PASSES, t=PACK))
+        load_scale_rows(0)
+        load_scale_rows(1)
+        load_plane(2)
+        load_scale_rows(2)
+        load_scale_rows(3)
+        for q in range(3, PASSES * PACK - 1):
+            load_plane(q)
+        nc.sync.dma_start(out=w_raw[:].bitcast(I32), in_=w_words.rearrange("z p c b -> p z (c b)").bitcast(I32))
+        load_plane(PASSES * PACK - 1)
+        nc.sync.dma_start(out=wb_raw[:], in_=wb.rearrange("(p t) n -> p t n", t=PACK))
+        nc.sync.dma_start(list3[:], offs3)
+        nc.sync.dma_start(list4[:], offs4)
+        nc.sync.dma_start(out=tz_sb[:], in_=tz.rearrange("(p h) z -> p h z", h=HALVES))
+
+        nc.gpsimd.memset(ws_raw[:].bitcast(U32), 0)
+        for quad in range(4):
+            live = slice(32 * quad, 32 * quad + 4)
+            nc.gpsimd.tensor_copy(out=ws_raw[live].bitcast(I32), in_=ws_rows[live])
+
+        w_codes = keep.tile([P, PASSES, R], U32, name="w_codes", align_bytes=64)
+        w_planes = keep.tile([P, PASSES, R], U8, name="w_planes", align_bytes=64)
+        for z in range(PASSES):
+            nc.vector.tensor_copy(
+                out=w_codes[:, z, :].rearrange("p (t c i) -> p c t i", t=PACK, i=4),
+                in_=w_raw[:, z, :].rearrange("p (c i t) -> p c t i", t=PACK, i=4),
+            )
+        nc.vector.tensor_copy(
+            out=w_planes[:].rearrange("p z (t m) -> p z t m", t=PACK),
+            in_=ws_raw[:].rearrange("p z (m t) -> p z t m", t=PACK),
+        )
+
+        acc = [psum.tile([P, J], F32, name=f"acc{t}") for t in range(PACK)]
+        for z in range(PASSES):
+            u_bf = keep.tile([P, J, PACK], BF16, name=f"u_bf{z}", tag=f"u_bf{z}", align_bytes=64)
+            u_codes = keep.tile([P, J], U32, name=f"u_codes{z}", align_bytes=64)
+            u_scales = keep.tile([P, J], U8, name=f"u_scales{z}", align_bytes=64)
+            last_pass = z == PASSES - 1
+            for t in range(PACK):
+                q = z * PACK + t
+                second = keep.tile([P, J], F32, name=f"second{q}")
+                gap = keep.tile([P, J], F32, name=f"gap{q}")
+                nc.scalar.activation(second[:], planes[q][:].indirect(list2[:]), COPY)
+                first = keep.tile([P, J], F32, name=f"first{q}")
+                if q in ON_SCALAR:
+                    nc.scalar.activation(first[:], planes[q][:].indirect(list1[:]), COPY)
+                else:
+                    nc.vector.tensor_copy(first[:], planes[q][:].indirect(list1[:]))
+                nc.vector.tensor_tensor(gap[:], first[:], second[:], SUB)
+                nc.vector.tensor_scalar(u_bf[:, :, t], gap[:], fk_sb[:, z, t : t + 1], None, MULT)
+            nc.vector.quantize_mx(
+                out=u_codes[:].bitcast(E4X4), scales=u_scales[:], in_=u_bf[:].rearrange("p j t -> p (j t)")
+            )
+            for t in range(PACK):
+                cols = slice(t * P, (t + 1) * P)
+                nc.tensor.matmul_mx(
+                    out=acc[t][:],
+                    lhsT=w_codes[:, z, cols].bitcast(E5X4),
+                    lhsT_scale=w_planes[:, z, cols],
+                    rhs=u_codes[:].bitcast(E4X4),
+                    rhs_scale=u_scales[:],
+                    start=(z == 0),
+                    stop=last_pass,
+                )
+
+        wb_bf = keep.tile([P, N, PACK], BF16, name="wb_bf", tag=f"plane{PASSES * PACK - 1}", align_bytes=64)
+        wb_codes = keep.tile([P, N], U32, name="wb_codes", tag=f"u_bf{PASSES - 1}", align_bytes=64)
+        wb_scales = keep.tile([P, N], U8, name="wb_scales", align_bytes=64)
+        nc.scalar.copy(
+            out=wb_bf[:].rearrange("p (h c e) t -> p c t e h", h=HALVES, e=2),
+            in_=wb_raw[:].rearrange("p t (c e h) -> p c t e h", h=HALVES, e=2),
+        )
+        nc.vector.quantize_mx(
+            out=wb_codes[:].bitcast(E5X4), scales=wb_scales[:], in_=wb_bf[:].rearrange("p n t -> p (n t)")
+        )
+        tz_picked = keep.tile([P, HALVES, O], F32, name="tz_picked", tag=f"plane{PASSES * PACK - 1}", align_bytes=64)
+        for h in range(HALVES):
+            nc.vector.tensor_copy(tz_picked[:, h, :], tz_sb[:, h, :].indirect(list4[:]))
+
+        hid_bf = keep.tile([P, O, PACK], BF16, name="hid_bf", align_bytes=64)
+        hid_codes = keep.tile([P, O], U32, name="hid_codes", align_bytes=64)
+        hid_scales = keep.tile([P, O], U8, name="hid_scales", align_bytes=64)
+        for t in range(PACK):
+            ha = keep.tile([P, J], F32, name=f"ha{t}")
+            nc.scalar.activation(ha[:], acc[t][:], RELU)
+            nc.vector.tensor_copy(hid_bf[:, :, t], ha[:].indirect(list3[:]))
+        nc.vector.quantize_mx(
+            out=hid_codes[:].bitcast(E5X4), scales=hid_scales[:], in_=hid_bf[:].rearrange("p o t -> p (o t)")
+        )
+        prod = psum.tile([P, HALVES, O], F32, name="prod")
+        for h in range(HALVES):
+            cols = slice(h * P, (h + 1) * P)
+            nc.tensor.matmul_mx(
+                out=prod[:, h, :],
+                lhsT=wb_codes[:, cols].bitcast(E5X4),
+                lhsT_scale=wb_scales[:, cols],
+                rhs=hid_codes[:].bitcast(E5X4),
+                rhs_scale=hid_scales[:],
+                start=True,
+                stop=True,
+            )
+        result = keep.tile([P, HALVES, O], F32, name="result")
+        nc.vector.tensor_tensor(result[:], prod[:], tz_picked[:], MULT)
+        nc.sync.dma_start(out=out.rearrange("(p h) o -> p h o", h=HALVES), in_=result[:])

@@ -21,8 +21,10 @@ RELU = mybir.ActivationFunctionType.Relu
 P = 128
 PACK = 4
 PASSES = K // (P * PACK)
+PLANES = PASSES * PACK
 HALVES = N // P
-ON_SCALAR = (1, 2, 3, 4, 5)
+RUN = 8
+GROUPS = ((0, 1), (2, 3), (4, 5, 6, 7))
 
 
 def tile_list_pickgaps_relooked_timeslook_kernel(tc, xf, fk, w_words, w_scales, wb, tz, offs, offs2, offs3, offs4, out):
@@ -35,17 +37,25 @@ def tile_list_pickgaps_relooked_timeslook_kernel(tc, xf, fk, w_words, w_scales, 
         list2 = keep.tile([P, J // 16], U16, name="list2")
         list3 = keep.tile([P, O // 16], U16, name="list3")
         list4 = keep.tile([P, O // 16], U16, name="list4")
-        fk_sb = keep.tile([P, PASSES, PACK], F32, name="fk_sb")
+        factors = [keep.tile([P, len(group)], F32, name=f"factors{group[0]}") for group in GROUPS]
         w_raw = keep.tile([P, PASSES, R], U32, name="w_raw")
-        ws_raw = keep.tile([P, PASSES, R], U8, name="ws_raw")
         ws_rows = keep.tile([P, PASSES, R // 4], I32, name="ws_rows")
         wb_raw = keep.tile([P, PACK, N], F32, name="wb_raw")
         tz_sb = keep.tile([P, HALVES, Z], F32, name="tz_sb")
-        planes = [keep.tile([P, T], F32, name=f"plane{q}", tag=f"plane{q}", align_bytes=64) for q in range(PASSES * PACK)]
+        planes = [keep.tile([P, T], F32, name=f"plane{q}", tag=f"plane{q}", align_bytes=64) for q in range(PLANES)]
         x_rows = xf.rearrange("(z p t) c -> z t p c", z=PASSES, t=PACK)
+        fk_rows = fk.rearrange("(z p t) one -> z p (t one)", z=PASSES, t=PACK)
+        wb_rows = wb.rearrange("(g t i) n -> t g i n", t=PACK, i=RUN)
+
+        warm = keep.tile([P, 2], F32, name="warm")
+        nc.vector.memset(warm[:, 0:1], 0.0)
+        nc.scalar.activation(warm[:, 1:2], warm[:, 0:1], COPY)
 
         def load_plane(q):
             nc.sync.dma_start(out=planes[q][:], in_=x_rows[q // PACK, q % PACK])
+
+        def load_factors(d):
+            nc.sync.dma_start(out=factors[d][:], in_=fk_rows[GROUPS[d][0] // PACK][:, GROUPS[d][0] % PACK : GROUPS[d][-1] % PACK + 1])
 
         def load_scale_rows(quad):
             nc.sync.dma_start(
@@ -57,72 +67,109 @@ def tile_list_pickgaps_relooked_timeslook_kernel(tc, xf, fk, w_words, w_scales, 
         nc.sync.dma_start(list2[:], offs2)
         nc.sync.dma_start(list1[:], offs)
         load_plane(1)
-        nc.sync.dma_start(out=fk_sb[:], in_=fk.rearrange("(z p t) one -> p z (t one)", z=PASSES, t=PACK))
         load_scale_rows(0)
         load_scale_rows(1)
         load_plane(2)
+        load_factors(0)
         load_scale_rows(2)
+        load_plane(3)
         load_scale_rows(3)
-        for q in range(3, PASSES * PACK - 1):
-            load_plane(q)
+        load_plane(4)
+        load_factors(1)
+        load_plane(5)
+        load_plane(6)
+        load_plane(7)
+        load_factors(2)
         nc.sync.dma_start(out=w_raw[:].bitcast(I32), in_=w_words.rearrange("z p c b -> p z (c b)").bitcast(I32))
-        load_plane(PASSES * PACK - 1)
-        nc.sync.dma_start(out=wb_raw[:], in_=wb.rearrange("(p t) n -> p t n", t=PACK))
         nc.sync.dma_start(list3[:], offs3)
+        for t in range(PACK):
+            nc.sync.dma_start(out=wb_raw[:, t, :], in_=wb_rows[t])
         nc.sync.dma_start(list4[:], offs4)
         nc.sync.dma_start(out=tz_sb[:], in_=tz.rearrange("(p h) z -> p h z", h=HALVES))
 
-        nc.gpsimd.memset(ws_raw[:].bitcast(U32), 0)
-        for quad in range(4):
-            live = slice(32 * quad, 32 * quad + 4)
-            nc.gpsimd.tensor_copy(out=ws_raw[live].bitcast(I32), in_=ws_rows[live])
-
         w_codes = keep.tile([P, PASSES, R], U32, name="w_codes", align_bytes=64)
         w_planes = keep.tile([P, PASSES, R], U8, name="w_planes", align_bytes=64)
-        for z in range(PASSES):
-            nc.vector.tensor_copy(
-                out=w_codes[:, z, :].rearrange("p (t c i) -> p c t i", t=PACK, i=4),
-                in_=w_raw[:, z, :].rearrange("p (c i t) -> p c t i", t=PACK, i=4),
+        nc.gpsimd.memset(w_planes[:].bitcast(U32), 0)
+        for quad in range(4):
+            live = slice(32 * quad, 32 * quad + 4)
+            nc.gpsimd.tensor_copy(
+                out=w_planes[live].bitcast(I32).rearrange("p z (t g i) -> p z t g i", t=PACK, i=RUN // 4),
+                in_=ws_rows[live].rearrange("p z (g t i) -> p z t g i", t=PACK, i=RUN // 4),
             )
-        nc.vector.tensor_copy(
-            out=w_planes[:].rearrange("p z (t m) -> p z t m", t=PACK),
-            in_=ws_raw[:].rearrange("p z (m t) -> p z t m", t=PACK),
-        )
+
+        def order_words(z):
+            nc.vector.tensor_copy(
+                out=w_codes[:, z, :].rearrange("p (t g i) -> p t g i", t=PACK, i=RUN),
+                in_=w_raw[:, z, :].rearrange("p (g t i) -> p t g i", t=PACK, i=RUN),
+            )
+
+        u_rows = [keep.tile([P, PACK, J], BF16, name=f"u_rows{z}") for z in range(PASSES)]
+        u_bf = [keep.tile([P, J, PACK], BF16, name=f"u_bf{z}", tag=f"u_bf{z}", align_bytes=64) for z in range(PASSES)]
+        u_codes = [keep.tile([P, J], U32, name=f"u_codes{z}", align_bytes=64) for z in range(PASSES)]
+        u_scales = [keep.tile([P, J], U8, name=f"u_scales{z}", align_bytes=64) for z in range(PASSES)]
+        gaps = []
+
+        def pick_gap(q):
+            second = keep.tile([P, J], F32, name=f"second{q}")
+            gap = keep.tile([P, J], F32, name=f"gap{q}", tag=f"gap{q}", align_bytes=64)
+            nc.scalar.activation(second[:], planes[q][:].indirect(list2[:]), COPY)
+            nc.vector.tensor_tensor(gap[:], planes[q][:].indirect(list1[:]), second[:], SUB)
+            gaps.append(gap)
+
+        def scale_group(d):
+            for e, q in enumerate(GROUPS[d]):
+                z, t = divmod(q, PACK)
+                nc.scalar.activation(u_rows[z][:, t, :], gaps[q][:], COPY, scale=factors[d][:, e : e + 1])
+
+        def interleave(z, slots):
+            nc.vector.tensor_copy(
+                out=u_bf[z][:, slots, :].rearrange("p (c i) t -> p c t i", i=4),
+                in_=u_rows[z][:, :, slots].rearrange("p t (c i) -> p c t i", i=4),
+            )
+
+        def quantise(z, slots):
+            nc.vector.quantize_mx(
+                out=u_codes[z][:, slots].bitcast(E4X4),
+                scales=u_scales[z][:, slots],
+                in_=u_bf[z][:, slots, :].rearrange("p j t -> p (j t)"),
+            )
+
+        whole = slice(0, J)
+        halves = (slice(0, J // 2), slice(J // 2, J))
+        for q in range(3):
+            pick_gap(q)
+        scale_group(0)
+        for q in range(3, 5):
+            pick_gap(q)
+        scale_group(1)
+        pick_gap(5)
+        interleave(0, whole)
+        pick_gap(6)
+        quantise(0, whole)
+        pick_gap(7)
+        scale_group(2)
+        order_words(0)
+        order_words(1)
+        for slots in halves:
+            interleave(1, slots)
+        for slots in halves:
+            quantise(1, slots)
 
         acc = [psum.tile([P, J], F32, name=f"acc{t}") for t in range(PACK)]
         for z in range(PASSES):
-            u_bf = keep.tile([P, J, PACK], BF16, name=f"u_bf{z}", tag=f"u_bf{z}", align_bytes=64)
-            u_codes = keep.tile([P, J], U32, name=f"u_codes{z}", align_bytes=64)
-            u_scales = keep.tile([P, J], U8, name=f"u_scales{z}", align_bytes=64)
-            last_pass = z == PASSES - 1
-            for t in range(PACK):
-                q = z * PACK + t
-                second = keep.tile([P, J], F32, name=f"second{q}")
-                gap = keep.tile([P, J], F32, name=f"gap{q}")
-                nc.scalar.activation(second[:], planes[q][:].indirect(list2[:]), COPY)
-                first = keep.tile([P, J], F32, name=f"first{q}")
-                if q in ON_SCALAR:
-                    nc.scalar.activation(first[:], planes[q][:].indirect(list1[:]), COPY)
-                else:
-                    nc.vector.tensor_copy(first[:], planes[q][:].indirect(list1[:]))
-                nc.vector.tensor_tensor(gap[:], first[:], second[:], SUB)
-                nc.vector.tensor_scalar(u_bf[:, :, t], gap[:], fk_sb[:, z, t : t + 1], None, MULT)
-            nc.vector.quantize_mx(
-                out=u_codes[:].bitcast(E4X4), scales=u_scales[:], in_=u_bf[:].rearrange("p j t -> p (j t)")
-            )
             for t in range(PACK):
                 cols = slice(t * P, (t + 1) * P)
                 nc.tensor.matmul_mx(
                     out=acc[t][:],
                     lhsT=w_codes[:, z, cols].bitcast(E5X4),
                     lhsT_scale=w_planes[:, z, cols],
-                    rhs=u_codes[:].bitcast(E4X4),
-                    rhs_scale=u_scales[:],
+                    rhs=u_codes[z][:].bitcast(E4X4),
+                    rhs_scale=u_scales[z][:],
                     start=(z == 0),
-                    stop=last_pass,
+                    stop=(z == PASSES - 1),
                 )
 
-        wb_bf = keep.tile([P, N, PACK], BF16, name="wb_bf", tag=f"plane{PASSES * PACK - 1}", align_bytes=64)
+        wb_bf = keep.tile([P, N, PACK], BF16, name="wb_bf", tag="gap7", align_bytes=64)
         wb_codes = keep.tile([P, N], U32, name="wb_codes", tag=f"u_bf{PASSES - 1}", align_bytes=64)
         wb_scales = keep.tile([P, N], U8, name="wb_scales", align_bytes=64)
         nc.scalar.copy(
@@ -132,20 +179,20 @@ def tile_list_pickgaps_relooked_timeslook_kernel(tc, xf, fk, w_words, w_scales, 
         nc.vector.quantize_mx(
             out=wb_codes[:].bitcast(E5X4), scales=wb_scales[:], in_=wb_bf[:].rearrange("p n t -> p (n t)")
         )
-        tz_picked = keep.tile([P, HALVES, O], F32, name="tz_picked", tag=f"plane{PASSES * PACK - 1}", align_bytes=64)
-        for h in range(HALVES):
-            nc.vector.tensor_copy(tz_picked[:, h, :], tz_sb[:, h, :].indirect(list4[:]))
 
         hid_bf = keep.tile([P, O, PACK], BF16, name="hid_bf", align_bytes=64)
         hid_codes = keep.tile([P, O], U32, name="hid_codes", align_bytes=64)
         hid_scales = keep.tile([P, O], U8, name="hid_scales", align_bytes=64)
         for t in range(PACK):
-            ha = keep.tile([P, J], F32, name=f"ha{t}")
+            ha = keep.tile([P, J], F32, name=f"ha{t}", tag=f"ha{t}")
             nc.scalar.activation(ha[:], acc[t][:], RELU)
             nc.vector.tensor_copy(hid_bf[:, :, t], ha[:].indirect(list3[:]))
         nc.vector.quantize_mx(
             out=hid_codes[:].bitcast(E5X4), scales=hid_scales[:], in_=hid_bf[:].rearrange("p o t -> p (o t)")
         )
+        tz_picked = keep.tile([P, HALVES, O], F32, name="tz_picked", tag="ha2")
+        for h in range(HALVES):
+            nc.scalar.activation(tz_picked[:, h, :], tz_sb[:, h, :].indirect(list4[:]), COPY)
         prod = psum.tile([P, HALVES, O], F32, name="prod")
         for h in range(HALVES):
             cols = slice(h * P, (h + 1) * P)

@@ -47,10 +47,6 @@ def tile_list_pickgaps_relooked_timeslook_kernel(tc, xf, fk, w_words, w_scales, 
         fk_rows = fk.rearrange("(z p t) one -> z p (t one)", z=PASSES, t=PACK)
         wb_rows = wb.rearrange("(g t i) n -> t g i n", t=PACK, i=RUN)
 
-        warm = keep.tile([P, 2], F32, name="warm")
-        nc.vector.memset(warm[:, 0:1], 0.0)
-        nc.scalar.activation(warm[:, 1:2], warm[:, 0:1], COPY)
-
         def load_plane(q):
             nc.sync.dma_start(out=planes[q][:], in_=x_rows[q // PACK, q % PACK])
 

from contextlib import ExitStack

import concourse.mybir as mybir

K, T, J, R, O, N, Z = 1024, 1024, 256, 512, 128, 256, 512
FLOPS = 2 * K * R * J + 2 * R * N * O

F32 = mybir.dt.float32
BF16 = mybir.dt.bfloat16
I32 = mybir.dt.int32
U32 = mybir.dt.uint32
U16 = mybir.dt.uint16
U8 = mybir.dt.uint8
E4X4 = mybir.dt.float8_e4m3fn_x4
E5X4 = mybir.dt.float8_e5m2_x4
MULT = mybir.AluOpType.mult
SUB = mybir.AluOpType.subtract
COPY = mybir.ActivationFunctionType.Copy
RELU = mybir.ActivationFunctionType.Relu

P = 128
PACK = 4
PASSES = K // (P * PACK)
PLANES = PASSES * PACK
HALVES = N // P
RUN = 8
GROUPS = ((0, 1), (2, 3), (4, 5, 6, 7))


def tile_list_pickgaps_relooked_timeslook_kernel(tc, xf, fk, w_words, w_scales, wb, tz, offs, offs2, offs3, offs4, out):
    nc = tc.nc
    with ExitStack() as ctx:
        keep = ctx.enter_context(tc.tile_pool(name="keep", bufs=1))
        psum = ctx.enter_context(tc.psum_pool(name="psum", bufs=1))

        list1 = keep.tile([P, J // 16], U16, name="list1")
        list2 = keep.tile([P, J // 16], U16, name="list2")
        list3 = keep.tile([P, O // 16], U16, name="list3")
        list4 = keep.tile([P, O // 16], U16, name="list4")
        factors = [keep.tile([P, len(group)], F32, name=f"factors{group[0]}") for group in GROUPS]
        w_raw = keep.tile([P, PASSES, R], U32, name="w_raw")
        ws_rows = keep.tile([P, PASSES, R // 4], I32, name="ws_rows")
        wb_raw = keep.tile([P, PACK, N], F32, name="wb_raw")
        tz_sb = keep.tile([P, HALVES, Z], F32, name="tz_sb")
        planes = [keep.tile([P, T], F32, name=f"plane{q}", tag=f"plane{q}", align_bytes=64) for q in range(PLANES)]
        x_rows = xf.rearrange("(z p t) c -> z t p c", z=PASSES, t=PACK)
        fk_rows = fk.rearrange("(z p t) one -> z p (t one)", z=PASSES, t=PACK)
        wb_rows = wb.rearrange("(g t i) n -> t g i n", t=PACK, i=RUN)

        def load_plane(q):
            nc.sync.dma_start(out=planes[q][:], in_=x_rows[q // PACK, q % PACK])

        def load_factors(d):
            nc.sync.dma_start(out=factors[d][:], in_=fk_rows[GROUPS[d][0] // PACK][:, GROUPS[d][0] % PACK : GROUPS[d][-1] % PACK + 1])

        def load_scale_rows(quad):
            nc.sync.dma_start(
                out=ws_rows[32 * quad : 32 * quad + 4],
                in_=w_scales[:, 4 * quad : 4 * quad + 4, :].rearrange("z q c -> q z c").bitcast(I32),
            )

        load_plane(0)
        nc.sync.dma_start(list2[:], offs2)
        nc.sync.dma_start(list1[:], offs)
        load_plane(1)
        load_scale_rows(0)
        load_scale_rows(1)
        load_plane(2)
        load_factors(0)
        load_scale_rows(2)
        load_plane(3)
        load_scale_rows(3)
        load_plane(4)
        load_factors(1)
        load_plane(5)
        load_plane(6)
        load_plane(7)
        load_factors(2)
        nc.sync.dma_start(out=w_raw[:].bitcast(I32), in_=w_words.rearrange("z p c b -> p z (c b)").bitcast(I32))
        nc.sync.dma_start(list3[:], offs3)
        for t in range(PACK):
            nc.sync.dma_start(out=wb_raw[:, t, :], in_=wb_rows[t])
        nc.sync.dma_start(list4[:], offs4)
        nc.sync.dma_start(out=tz_sb[:], in_=tz.rearrange("(p h) z -> p h z", h=HALVES))

        w_codes = keep.tile([P, PASSES, R], U32, name="w_codes", align_bytes=64)
        w_planes = keep.tile([P, PASSES, R], U8, name="w_planes", align_bytes=64)
        nc.gpsimd.memset(w_planes[:].bitcast(U32), 0)
        for quad in range(4):
            live = slice(32 * quad, 32 * quad + 4)
            nc.gpsimd.tensor_copy(
                out=w_planes[live].bitcast(I32).rearrange("p z (t g i) -> p z t g i", t=PACK, i=RUN // 4),
                in_=ws_rows[live].rearrange("p z (g t i) -> p z t g i", t=PACK, i=RUN // 4),
            )

        def order_words(z):
            nc.vector.tensor_copy(
                out=w_codes[:, z, :].rearrange("p (t g i) -> p t g i", t=PACK, i=RUN),
                in_=w_raw[:, z, :].rearrange("p (g t i) -> p t g i", t=PACK, i=RUN),
            )

        u_rows = [keep.tile([P, PACK, J], BF16, name=f"u_rows{z}") for z in range(PASSES)]
        u_bf = [keep.tile([P, J, PACK], BF16, name=f"u_bf{z}", tag=f"u_bf{z}", align_bytes=64) for z in range(PASSES)]
        u_codes = [keep.tile([P, J], U32, name=f"u_codes{z}", align_bytes=64) for z in range(PASSES)]
        u_scales = [keep.tile([P, J], U8, name=f"u_scales{z}", align_bytes=64) for z in range(PASSES)]
        gaps = []

        def pick_gap(q):
            second = keep.tile([P, J], F32, name=f"second{q}")
            gap = keep.tile([P, J], F32, name=f"gap{q}", tag=f"gap{q}", align_bytes=64)
            nc.scalar.activation(second[:], planes[q][:].indirect(list2[:]), COPY)
            nc.vector.tensor_tensor(gap[:], planes[q][:].indirect(list1[:]), second[:], SUB)
            gaps.append(gap)

        def scale_group(d):
            for e, q in enumerate(GROUPS[d]):
                z, t = divmod(q, PACK)
                nc.scalar.activation(u_rows[z][:, t, :], gaps[q][:], COPY, scale=factors[d][:, e : e + 1])

        def interleave(z, slots):
            nc.vector.tensor_copy(
                out=u_bf[z][:, slots, :].rearrange("p (c i) t -> p c t i", i=4),
                in_=u_rows[z][:, :, slots].rearrange("p t (c i) -> p c t i", i=4),
            )

        def quantise(z, slots):
            nc.vector.quantize_mx(
                out=u_codes[z][:, slots].bitcast(E4X4),
                scales=u_scales[z][:, slots],
                in_=u_bf[z][:, slots, :].rearrange("p j t -> p (j t)"),
            )

        whole = slice(0, J)
        halves = (slice(0, J // 2), slice(J // 2, J))
        for q in range(3):
            pick_gap(q)
        scale_group(0)
        for q in range(3, 5):
            pick_gap(q)
        scale_group(1)
        pick_gap(5)
        interleave(0, whole)
        pick_gap(6)
        quantise(0, whole)
        pick_gap(7)
        scale_group(2)
        order_words(0)
        order_words(1)
        for slots in halves:
            interleave(1, slots)
        for slots in halves:
            quantise(1, slots)

        acc = [psum.tile([P, J], F32, name=f"acc{t}") for t in range(PACK)]
        for z in range(PASSES):
            for t in range(PACK):
                cols = slice(t * P, (t + 1) * P)
                nc.tensor.matmul_mx(
                    out=acc[t][:],
                    lhsT=w_codes[:, z, cols].bitcast(E5X4),
                    lhsT_scale=w_planes[:, z, cols],
                    rhs=u_codes[z][:].bitcast(E4X4),
                    rhs_scale=u_scales[z][:],
                    start=(z == 0),
                    stop=(z == PASSES - 1),
                )

        wb_bf = keep.tile([P, N, PACK], BF16, name="wb_bf", tag="gap7", align_bytes=64)
        wb_codes = keep.tile([P, N], U32, name="wb_codes", tag=f"u_bf{PASSES - 1}", align_bytes=64)
        wb_scales = keep.tile([P, N], U8, name="wb_scales", align_bytes=64)
        nc.scalar.copy(
            out=wb_bf[:].rearrange("p (h c e) t -> p c t e h", h=HALVES, e=2),
            in_=wb_raw[:].rearrange("p t (c e h) -> p c t e h", h=HALVES, e=2),
        )
        nc.vector.quantize_mx(
            out=wb_codes[:].bitcast(E5X4), scales=wb_scales[:], in_=wb_bf[:].rearrange("p n t -> p (n t)")
        )

        hid_bf = keep.tile([P, O, PACK], BF16, name="hid_bf", align_bytes=64)
        hid_codes = keep.tile([P, O], U32, name="hid_codes", align_bytes=64)
        hid_scales = keep.tile([P, O], U8, name="hid_scales", align_bytes=64)
        for t in range(PACK):
            ha = keep.tile([P, J], F32, name=f"ha{t}", tag=f"ha{t}")
            nc.scalar.activation(ha[:], acc[t][:], RELU)
            nc.vector.tensor_copy(hid_bf[:, :, t], ha[:].indirect(list3[:]))
        nc.vector.quantize_mx(
            out=hid_codes[:].bitcast(E5X4), scales=hid_scales[:], in_=hid_bf[:].rearrange("p o t -> p (o t)")
        )
        tz_picked = keep.tile([P, HALVES, O], F32, name="tz_picked", tag="ha2")
        for h in range(HALVES):
            nc.scalar.activation(tz_picked[:, h, :], tz_sb[:, h, :].indirect(list4[:]), COPY)
        prod = psum.tile([P, HALVES, O], F32, name="prod")
        for h in range(HALVES):
            cols = slice(h * P, (h + 1) * P)
            nc.tensor.matmul_mx(
                out=prod[:, h, :],
                lhsT=wb_codes[:, cols].bitcast(E5X4),
                lhsT_scale=wb_scales[:, cols],
                rhs=hid_codes[:].bitcast(E5X4),
                rhs_scale=hid_scales[:],
                start=True,
                stop=True,
            )
        result = keep.tile([P, HALVES, O], F32, name="result")
        nc.vector.tensor_tensor(result[:], prod[:], tz_picked[:], MULT)
        nc.sync.dma_start(out=out.rearrange("(p h) o -> p h o", h=HALVES), in_=result[:])
